import numpy as np
import ml_dtypes


def mxq(x, axis, fmt="e4m3"):
    dtype, down = {"e4m3": (ml_dtypes.float8_e4m3fn, 7), "e5m2": (ml_dtypes.float8_e5m2, 14)}[fmt]
    v = np.moveaxis(np.asarray(x, np.float32).astype(ml_dtypes.bfloat16).astype(np.float64), axis, -1)
    blocks = v.reshape(v.shape[:-1] + (-1, 32))
    amax = np.abs(blocks).max(-1, keepdims=True)
    byte = np.maximum(np.where(amax > 0, np.frexp(amax)[1] - 1 + 127, 0) - down, 1)
    scale = np.exp2(byte - 127.0)
    codes = (blocks / scale).astype(np.float32).astype(dtype).astype(np.float64)
    return np.moveaxis((codes * scale).reshape(v.shape), -1, axis)


WIDE = False


def mx_kscale(k):
    if not WIDE:
        return np.ones(k)
    levels = np.array([10, -10, 5, -5, 0])
    if k % 512:
        return np.exp2(np.random.permutation(np.resize(levels, k // 32))).repeat(32)
    a = np.empty((k // 512, 16))
    for p in range(k // 512):
        a[p, :8] = np.random.permutation(np.resize(levels, 8))
        for g in range(8):
            far = levels[np.abs(levels - a[p, g]) >= 10]
            a[p, g + 8] = far[np.random.randint(len(far))]
    return np.exp2(a.ravel()).repeat(32)


def f64(x):
    return np.asarray(x).astype(np.float64)


def striped(idx):
    return np.tile(np.asarray(idx).reshape(-1, 16).T, (8, 1)).astype(np.uint16)


def unstriped(offs):
    return offs[:16].T.reshape(-1).astype(np.int64)


def striped8(idx):
    return np.asarray(idx).reshape(8, -1, 16).transpose(0, 2, 1).reshape(128, -1).astype(np.uint16)


def unstriped8(offs):
    return offs.reshape(8, 16, -1).transpose(0, 2, 1).reshape(8, -1).astype(np.int64)


def pick8(x, idx, run):
    r = np.arange(len(x))
    return x[r[:, None], idx[r % (8 * run) // run]]


E2M1 = np.array([0.0, 0.5, 1.0, 1.5, 2.0, 3.0, 4.0, 6.0, -0.0, -0.5, -1.0, -1.5, -2.0, -3.0, -4.0, -6.0])


def pack_weight(w, fmt):
    k, n = w.shape
    w = f64(np.asarray(w, np.float32).astype(ml_dtypes.bfloat16)).reshape(k // 32, 32, n)
    amax = np.abs(w).max(1)
    if fmt == "e4m3":
        byte = np.frexp(amax)[1] - 1 + 127 - 7
    else:
        mant, ex = np.frexp(amax / 6.0)
        byte = np.where(mant > 0.5, ex, ex - 1) + 127
    byte = np.clip(np.where(amax > 0, byte, 1), 1, 254)
    scaled = (w * np.exp2(127.0 - byte)[:, None, :]).reshape(k, n).astype(np.float32)
    by_word = np.ascontiguousarray(scaled.reshape(k // 512, 128, 4, n).transpose(0, 1, 3, 2))
    if fmt == "e4m3":
        words = by_word.astype(ml_dtypes.float8_e4m3fn).view(np.uint8)
    else:
        c = by_word.astype(ml_dtypes.float4_e2m1fn).view(np.uint8) & 0xF
        words = (c[..., 0::2] | (c[..., 1::2] << 4)).reshape(k // 512, 128, 2 * n)
    return np.ascontiguousarray(words), np.ascontiguousarray(byte.astype(np.uint8).reshape(k // 512, 16, n))


def unpack_weight(words, scales, fmt):
    g, _, n = scales.shape
    words = np.ascontiguousarray(words).reshape(g, 128, n, -1)
    if fmt == "e4m3":
        vals = words.view(ml_dtypes.float8_e4m3fn).astype(np.float64)
    else:
        nib = np.empty((g, 128, n, 4), np.uint8)
        nib[..., 0::2] = words & 0xF
        nib[..., 1::2] = words >> 4
        vals = E2M1[nib]
    vals = vals * np.repeat(np.exp2(scales.astype(np.float64) - 127.0), 8, axis=1)[..., None]
    return vals.transpose(0, 1, 3, 2).reshape(g * 512, n)


K, J, R, T, F, Z, M, C, O, N, S = 512, 256, 512, 512, 2048, 512, 1024, 512, 128, 256, 1024


def setup_inputs():
    n = np.random.standard_normal
    idx = np.random.permutation(T)[:J]
    idx2 = np.stack([np.random.permutation(F)[:R] for _ in range(8)])
    idx3 = np.random.permutation(M)[:J]
    idx4 = np.random.permutation(C)[:J]
    idx5 = np.random.permutation(C)[:O]
    idx6 = np.stack([np.random.permutation(C)[:O] for _ in range(8)])
    idx7 = np.random.permutation(S)[:N]
    fk = mx_kscale(K)
    fz = mx_kscale(Z)
    fr = mx_kscale(R)
    xtp = pack_weight(n((K, T)) * fk[:, None], "e4m3")
    xop = pack_weight(n((Z, M)) / fz[:, None], "e2m1")
    w2p = pack_weight(n((Z, R)) * 1 / np.sqrt(Z) * fz[:, None], "e4m3")
    vsp = pack_weight(n((R, S)) * 1 / np.sqrt(R) / fr[:, None], "e4m3")
    return {
        "xt_words": xtp[0],
        "xt_scales": xtp[1],
        "ua": (np.random.randint(-7, 8, (K, F)).astype(np.float64)).astype(np.float32),
        "ha": ((np.random.randint(8, 25, (K, 1)) / 1024.0) / fk[:, None]).astype(np.float32),
        "xo_words": xop[0],
        "xo_scales": xop[1],
        "w2_words": w2p[0],
        "w2_scales": w2p[1],
        "sa": (np.random.uniform(0.5, 1.6, (R, 1)) * fr[:, None]).astype(np.float32),
        "sb": (np.random.uniform(0.5, 1.6, (R, 1)) * fr[:, None]).astype(np.float32),
        "vs_words": vsp[0],
        "vs_scales": vsp[1],
        "offs": striped(idx),
        "offs2": striped8(idx2),
        "offs3": striped(idx3),
        "offs4": striped(idx4),
        "offs5": striped(idx5),
        "offs6": striped8(idx6),
        "offs7": striped(idx7),
    }


def reference(xt_words, xt_scales, ua, ha, xo_words, xo_scales, w2_words, w2_scales, sa, sb, vs_words, vs_scales, offs, offs2, offs3, offs4, offs5, offs6, offs7):
    idx = unstriped(offs)
    idx2 = unstriped8(offs2)
    idx3 = unstriped(offs3)
    idx4 = unstriped(offs4)
    idx5 = unstriped(offs5)
    idx6 = unstriped8(offs6)
    idx7 = unstriped(offs7)
    xtu = unpack_weight(xt_words, xt_scales, "e4m3")
    xou = unpack_weight(xo_words, xo_scales, "e2m1")
    w2u = unpack_weight(w2_words, w2_scales, "e4m3")
    vsu = unpack_weight(vs_words, vs_scales, "e4m3")
    wc = pick8(f64(ua), idx2, 64) * f64(ha)
    wcq = mxq(wc, 0, "e4m3")
    xtidxg = xtu[:, idx]
    xoidx3g = xou[:, idx3]
    a = wcq.T @ xtidxg + w2u.T @ xoidx3g
    pw = np.zeros((R, C))
    pw[:, idx4] = a
    hid = np.maximum(pw[:, idx5] * f64(sa), pick8(pw, idx6, 64) * f64(sb))
    vsidx7g = vsu[:, idx7]
    hidq = mxq(hid, 0, "e4m3")
    y = vsidx7g.T @ hidq
    return y

@@ -1,0 +1,200 @@
+from contextlib import ExitStack
+
+import concourse.mybir as mybir
+
+K, J, R, T, F, M, C, O, N, S = 512, 256, 512, 512, 2048, 1024, 512, 128, 256, 1024
+FLOPS = 2 * (K * R * J + 512 * R * J + R * N * O)
+
+F32 = mybir.dt.float32
+BF16 = mybir.dt.bfloat16
+I32 = mybir.dt.int32
+U32 = mybir.dt.uint32
+U16 = mybir.dt.uint16
+U8 = mybir.dt.uint8
+FP8X4 = mybir.dt.float8_e4m3fn_x4
+FP4X4 = mybir.dt.float4_e2m1fn_x4
+COPY = mybir.ActivationFunctionType.Copy
+MAX = mybir.AluOpType.max
+
+P = 128
+PACK = 4
+
+
+def tile_picked_tokens_codes_bank_boardmixed_store_plain_kernel(
+    tc, xt_words, xt_scales, ua, ha, xo_words, xo_scales, w2_words, w2_scales, sa, sb, vs_words, vs_scales,
+    offs, offs2, offs3, offs4, offs5, offs6, offs7, out,
+):
+    nc = tc.nc
+    with ExitStack() as ctx:
+        keep = ctx.enter_context(tc.tile_pool(name="keep", bufs=1))
+        psum = ctx.enter_context(tc.psum_pool(name="psum", bufs=1))
+
+        def load_list(src, name):
+            tile = keep.tile(list(src.shape), U16, name=name)
+            nc.sync.dma_start(tile[:], src)
+            return tile
+
+        def load_column(src, name):
+            tile = keep.tile([P, PACK], F32, name=name)
+            nc.sync.dma_start(tile[:], src.rearrange("(p t) o -> p (t o)", t=PACK))
+            return tile
+
+        def load_words(src, dtype, width, name):
+            tile = keep.tile([P, width], dtype, name=name, align_bytes=64)
+            nc.sync.dma_start(tile[:].bitcast(I32), src.bitcast(I32))
+            return tile
+
+        def load_scale_rows(src, width, name):
+            tile = keep.tile([PACK, PACK, width // 4], I32, name=name)
+            nc.sync.dma_start(tile[:], src[0].bitcast(I32).rearrange("(q i) w -> i q w", i=PACK))
+            return tile
+
+        def zeroed_plane(width, name):
+            plane = keep.tile([P, width], U8, name=name, align_bytes=64)
+            nc.vector.memset(plane[:].bitcast(I32), 0)
+            return plane
+
+        def spread_scale_rows(plane, rows):
+            for q in range(PACK):
+                nc.vector.tensor_copy(plane[:].bitcast(I32)[32 * q : 32 * q + PACK, :], rows[:, q, :])
+
+        def gather(window, offsets, dtype, name):
+            picked = keep.tile([P, 16 * offsets.shape[1]], dtype, name=name, align_bytes=64)
+            nc.vector.tensor_copy(picked[:], window[:].indirect(offsets[:]))
+            return picked
+
+        ua_rows = ua.rearrange("(p t) f -> t p f", t=PACK)
+
+        def load_ua(t):
+            tile = keep.tile([P, F], F32, name="ua%d" % t)
+            nc.sync.dma_start(tile[:], ua_rows[t])
+            return tile
+
+        e4m3_words = "p n t -> p (n t)"
+        list2 = load_list(offs2, "list2")
+        ha_t = load_column(ha, "ha_t")
+        ua_tiles = [load_ua(0)]
+        xo_rows = load_scale_rows(xo_scales, M, "xo_rows")
+        xt_rows = load_scale_rows(xt_scales, T, "xt_rows")
+        w2_rows = load_scale_rows(w2_scales, R, "w2_rows")
+        list3 = load_list(offs3, "list3")
+        list1 = load_list(offs, "list1")
+        ua_tiles.append(load_ua(1))
+        xo_all = load_words(xo_words[0], U16, M, "xo_all")
+        xt_all = load_words(xt_words[0].rearrange(e4m3_words), U32, T, "xt_all")
+        ua_tiles.append(load_ua(2))
+        w2_all = load_words(w2_words[0].rearrange(e4m3_words), U32, R, "w2_all")
+        ua_tiles.append(load_ua(3))
+        list4 = load_list(offs4, "list4")
+        vs_rows = load_scale_rows(vs_scales, S, "vs_rows")
+        sa_t = load_column(sa, "sa_t")
+        sb_t = load_column(sb, "sb_t")
+        list5 = load_list(offs5, "list5")
+        list6 = load_list(offs6, "list6")
+        list7 = load_list(offs7, "list7")
+        vs_all = load_words(vs_words[0].rearrange(e4m3_words), U32, S, "vs_all")
+
+        xo_plane = zeroed_plane(M, "xo_plane")
+        xt_plane = zeroed_plane(T, "xt_plane")
+        w2_plane = zeroed_plane(R, "w2_plane")
+        vs_plane = zeroed_plane(S, "vs_plane")
+        board = [keep.tile([P, C], F32, name="board%d" % t) for t in range(PACK)]
+        for t in range(PACK):
+            nc.vector.memset(board[t][:], 0.0)
+
+        spread_scale_rows(xo_plane, xo_rows)
+        spread_scale_rows(xt_plane, xt_rows)
+        spread_scale_rows(w2_plane, w2_rows)
+        xo_s = gather(xo_plane, list3, U8, "xo_s")
+        xt_s = gather(xt_plane, list1, U8, "xt_s")
+        w2_s = keep.tile([P, PACK, P], U8, name="w2_s", align_bytes=64)
+        nc.vector.tensor_copy(w2_s[:], w2_plane[:].rearrange("p (m t) -> p t m", t=PACK))
+
+        wc_planes = keep.tile([P, PACK, R], BF16, name="wc_planes")
+        wc_in = [keep.tile([P, P, PACK], BF16, name="wc_in%d" % u, align_bytes=64) for u in range(PACK)]
+
+        def fetch_wc(t):
+            nc.scalar.activation(wc_planes[:, t, :], ua_tiles[t][:].indirect(list2[:]), COPY, scale=ha_t[:, t : t + 1])
+
+        def place_wc(t, u):
+            nc.vector.tensor_copy(wc_in[u][:, :, t], wc_planes[:, t, :].rearrange("p (m u) -> p u m", u=PACK)[:, u, :])
+
+        fetch_wc(0)
+        for u in range(PACK):
+            place_wc(0, u)
+        xo_w = gather(xo_all, list3, U16, "xo_w")
+        fetch_wc(1)
+        for u in range(PACK):
+            place_wc(1, u)
+        xt_w = gather(xt_all, list1, U32, "xt_w")
+        fetch_wc(2)
+        for u in range(PACK):
+            place_wc(2, u)
+        w2_w = keep.tile([P, PACK, P], I32, name="w2_w", align_bytes=64)
+        nc.vector.tensor_copy(w2_w[:], w2_all[:].bitcast(I32).rearrange("p (m t) -> p t m", t=PACK))
+
+        acc = [psum.tile([P, J], F32, name="acc%d" % u) for u in range(PACK)]
+        for u in range(PACK):
+            nc.tensor.matmul_mx(acc[u][:], lhsT=w2_w[:, u, :].bitcast(FP8X4), lhsT_scale=w2_s[:, u, :],
+                                rhs=xo_w[:].bitcast(FP4X4), rhs_scale=xo_s[:], start=True, stop=False)
+
+        fetch_wc(3)
+        wc_w = [keep.tile([P, P], U32, name="wc_w%d" % u, align_bytes=64) for u in range(PACK)]
+        wc_s = [keep.tile([P, P], U8, name="wc_s%d" % u, align_bytes=64) for u in range(PACK)]
+        a_sb = [keep.tile([P, J], F32, name="a_sb%d" % u) for u in range(PACK)]
+
+        def first_product(u):
+            nc.vector.quantize_mx(wc_w[u][:].bitcast(FP8X4), wc_s[u][:], wc_in[u][:].rearrange("p m t -> p (m t)"))
+            nc.tensor.matmul_mx(acc[u][:], lhsT=wc_w[u][:].bitcast(FP8X4), lhsT_scale=wc_s[u][:],
+                                rhs=xt_w[:].bitcast(FP8X4), rhs_scale=xt_s[:], start=False, stop=True)
+            nc.scalar.copy(a_sb[u][:], acc[u][:])
+
+        place_wc(3, 0)
+        for u in range(PACK):
+            if u + 1 < PACK:
+                place_wc(3, u + 1)
+            first_product(u)
+
+        one = keep.tile([P, PACK, O], F32, name="one")
+        eight = keep.tile([P, PACK, O], F32, name="eight")
+        hid_in = keep.tile([P, O, PACK], BF16, name="hid_in", align_bytes=64)
+
+        def scatter(u, engine, lo=0, hi=J):
+            window = board[u][:].indirect(list4[:, lo // 16 : hi // 16])
+            if engine == "vector":
+                nc.vector.tensor_copy(window, a_sb[u][:, lo:hi])
+            else:
+                nc.scalar.activation(window, a_sb[u][:, lo:hi], COPY)
+
+        def read_board(u):
+            nc.scalar.activation(one[:, u, :], board[u][:].indirect(list5[:]), COPY, scale=sa_t[:, u : u + 1])
+            nc.scalar.activation(eight[:, u, :], board[u][:].indirect(list6[:]), COPY, scale=sb_t[:, u : u + 1])
+
+        def larger(u):
+            nc.vector.tensor_tensor(hid_in[:, :, u], one[:, u, :], eight[:, u, :], MAX)
+
+        scatter(0, "vector")
+        scatter(3, "scalar")
+        spread_scale_rows(vs_plane, vs_rows)
+        scatter(1, "vector")
+        read_board(0)
+        read_board(3)
+        scatter(2, "vector")
+        read_board(1)
+        vs_s = gather(vs_plane, list7, U8, "vs_s")
+        vs_w = gather(vs_all, list7, U32, "vs_w")
+        read_board(2)
+        for u in (0, 3, 1, 2):
+            larger(u)
+
+        hid_w = keep.tile([P, O], U32, name="hid_w", align_bytes=64)
+        hid_s = keep.tile([P, O], U8, name="hid_s", align_bytes=64)
+        nc.vector.quantize_mx(hid_w[:].bitcast(FP8X4), hid_s[:], hid_in[:].rearrange("p o t -> p (o t)"))
+        y = psum.tile([P, N // P, O], F32, name="y")
+        for h in range(N // P):
+            cols = slice(h * P, (h + 1) * P)
+            nc.tensor.matmul_mx(y[:, h, :], lhsT=vs_w[:, cols].bitcast(FP8X4), lhsT_scale=vs_s[:, cols],
+                                rhs=hid_w[:].bitcast(FP8X4), rhs_scale=hid_s[:], start=True, stop=True)
+        y_sb = keep.tile([P, N // P, O], F32, name="y_sb")
+        nc.vector.tensor_copy(y_sb[:], y[:])
+        nc.sync.dma_start(out.rearrange("(h p) o -> p h o", p=P), y_sb[:])

@@ -18,6 +18,7 @@ MAX = mybir.AluOpType.max
 
 P = 128
 PACK = 4
+QUAD = 32
 
 
 def tile_picked_tokens_codes_bank_boardmixed_store_plain_kernel(
@@ -40,26 +41,25 @@ def tile_picked_tokens_codes_bank_boardmixed_store_plain_kernel(
             return tile
 
         def load_words(src, dtype, width, name):
-            tile = keep.tile([P, width], dtype, name=name, align_bytes=64)
+            tile = keep.tile([P, width], dtype, name=name, tag=name, align_bytes=64)
             nc.sync.dma_start(tile[:].bitcast(I32), src.bitcast(I32))
             return tile
 
-        def load_scale_rows(src, width, name):
-            tile = keep.tile([PACK, PACK, width // 4], I32, name=name)
-            nc.sync.dma_start(tile[:], src[0].bitcast(I32).rearrange("(q i) w -> i q w", i=PACK))
-            return tile
+        def load_scale_rows(src, width, first, name):
+            tile = keep.tile([P, PACK, width // 4], I32, name=name)
+            base = first // QUAD * QUAD
+            nc.vector.memset(tile[base : base + QUAD], 0)
+            nc.scalar.dma_start(tile[first : first + PACK], src[0].bitcast(I32).rearrange("(q i) w -> i q w", i=PACK))
+            return tile[base : base + QUAD]
 
-        def zeroed_plane(width, name):
-            plane = keep.tile([P, width], U8, name=name, align_bytes=64)
-            nc.vector.memset(plane[:].bitcast(I32), 0)
+        def spread_scale_rows(rows, name):
+            plane = keep.tile([P, 4 * rows.shape[2]], U8, name=name, align_bytes=64)
+            for q in range(PACK):
+                nc.vector.tensor_copy(plane[:].bitcast(I32)[QUAD * q : QUAD * (q + 1), :], rows[:, q, :])
             return plane
 
-        def spread_scale_rows(plane, rows):
-            for q in range(PACK):
-                nc.vector.tensor_copy(plane[:].bitcast(I32)[32 * q : 32 * q + PACK, :], rows[:, q, :])
-
-        def gather(window, offsets, dtype, name):
-            picked = keep.tile([P, 16 * offsets.shape[1]], dtype, name=name, align_bytes=64)
+        def gather(window, offsets, dtype, name, tag=None):
+            picked = keep.tile([P, 16 * offsets.shape[1]], dtype, name=name, tag=tag or name, align_bytes=64)
             nc.vector.tensor_copy(picked[:], window[:].indirect(offsets[:]))
             return picked
 
@@ -70,94 +70,94 @@ def tile_picked_tokens_codes_bank_boardmixed_store_plain_kernel(
             nc.sync.dma_start(tile[:], ua_rows[t])
             return tile
 
+        XO0, W20, XT0, VS0 = 0, 64, 4, 8
         e4m3_words = "p n t -> p (n t)"
+        xo_rows = load_scale_rows(xo_scales, M, XO0, "xo_rows")
+        w2_rows = load_scale_rows(w2_scales, R, W20, "w2_rows")
+        xt_rows = load_scale_rows(xt_scales, T, XT0, "xt_rows")
+        vs_rows = load_scale_rows(vs_scales, S, VS0, "vs_rows")
+        ua_tiles = [load_ua(0)]
         list2 = load_list(offs2, "list2")
         ha_t = load_column(ha, "ha_t")
-        ua_tiles = [load_ua(0)]
-        xo_rows = load_scale_rows(xo_scales, M, "xo_rows")
-        xt_rows = load_scale_rows(xt_scales, T, "xt_rows")
-        w2_rows = load_scale_rows(w2_scales, R, "w2_rows")
         list3 = load_list(offs3, "list3")
         list1 = load_list(offs, "list1")
+        list7 = load_list(offs7, "list7")
         ua_tiles.append(load_ua(1))
         xo_all = load_words(xo_words[0], U16, M, "xo_all")
-        xt_all = load_words(xt_words[0].rearrange(e4m3_words), U32, T, "xt_all")
-        ua_tiles.append(load_ua(2))
         w2_all = load_words(w2_words[0].rearrange(e4m3_words), U32, R, "w2_all")
+        ua_tiles.append(load_ua(2))
         ua_tiles.append(load_ua(3))
+        xt_all = load_words(xt_words[0].rearrange(e4m3_words), U32, T, "xt_all")
         list4 = load_list(offs4, "list4")
-        vs_rows = load_scale_rows(vs_scales, S, "vs_rows")
         sa_t = load_column(sa, "sa_t")
         sb_t = load_column(sb, "sb_t")
         list5 = load_list(offs5, "list5")
         list6 = load_list(offs6, "list6")
-        list7 = load_list(offs7, "list7")
         vs_all = load_words(vs_words[0].rearrange(e4m3_words), U32, S, "vs_all")
 
-        xo_plane = zeroed_plane(M, "xo_plane")
-        xt_plane = zeroed_plane(T, "xt_plane")
-        w2_plane = zeroed_plane(R, "w2_plane")
-        vs_plane = zeroed_plane(S, "vs_plane")
         board = [keep.tile([P, C], F32, name="board%d" % t) for t in range(PACK)]
         for t in range(PACK):
             nc.vector.memset(board[t][:], 0.0)
 
-        spread_scale_rows(xo_plane, xo_rows)
-        spread_scale_rows(xt_plane, xt_rows)
-        spread_scale_rows(w2_plane, w2_rows)
-        xo_s = gather(xo_plane, list3, U8, "xo_s")
-        xt_s = gather(xt_plane, list1, U8, "xt_s")
+        xo_s = gather(spread_scale_rows(xo_rows, "xo_plane"), list3, U8, "xo_s")
+        w2_plane = spread_scale_rows(w2_rows, "w2_plane")
         w2_s = keep.tile([P, PACK, P], U8, name="w2_s", align_bytes=64)
         nc.vector.tensor_copy(w2_s[:], w2_plane[:].rearrange("p (m t) -> p t m", t=PACK))
+        xt_s = gather(spread_scale_rows(xt_rows, "xt_plane"), list1, U8, "xt_s")
+        vs_s = gather(spread_scale_rows(vs_rows, "vs_plane"), list7, U8, "vs_s")
 
         wc_planes = keep.tile([P, PACK, R], BF16, name="wc_planes")
         wc_in = [keep.tile([P, P, PACK], BF16, name="wc_in%d" % u, align_bytes=64) for u in range(PACK)]
+        dealt = wc_planes[:].rearrange("p t (m u) -> p u m t", u=PACK)
 
         def fetch_wc(t):
             nc.scalar.activation(wc_planes[:, t, :], ua_tiles[t][:].indirect(list2[:]), COPY, scale=ha_t[:, t : t + 1])
 
-        def place_wc(t, u):
-            nc.vector.tensor_copy(wc_in[u][:, :, t], wc_planes[:, t, :].rearrange("p (m u) -> p u m", u=PACK)[:, u, :])
+        def place_wc(copy, u, lo, hi):
+            copy(wc_in[u][:, :, lo:hi], dealt[:, u, :, lo:hi])
 
         fetch_wc(0)
-        for u in range(PACK):
-            place_wc(0, u)
         xo_w = gather(xo_all, list3, U16, "xo_w")
         fetch_wc(1)
         for u in range(PACK):
-            place_wc(1, u)
-        xt_w = gather(xt_all, list1, U32, "xt_w")
-        fetch_wc(2)
-        for u in range(PACK):
-            place_wc(2, u)
+            place_wc(nc.vector.tensor_copy, u, 0, 2)
         w2_w = keep.tile([P, PACK, P], I32, name="w2_w", align_bytes=64)
-        nc.vector.tensor_copy(w2_w[:], w2_all[:].bitcast(I32).rearrange("p (m t) -> p t m", t=PACK))
-
+        nc.vector.tensor_copy(
+            w2_w[:].rearrange("p t (a m) -> p a t m", m=PACK),
+            w2_all[:].bitcast(I32).rearrange("p (a m t) -> p a t m", m=PACK, t=PACK),
+        )
         acc = [psum.tile([P, J], F32, name="acc%d" % u) for u in range(PACK)]
         for u in range(PACK):
             nc.tensor.matmul_mx(acc[u][:], lhsT=w2_w[:, u, :].bitcast(FP8X4), lhsT_scale=w2_s[:, u, :],
                                 rhs=xo_w[:].bitcast(FP4X4), rhs_scale=xo_s[:], start=True, stop=False)
-
+        fetch_wc(2)
+        for u in range(2):
+            place_wc(nc.vector.tensor_copy, u, 2, 3)
+        xt_w = gather(xt_all, list1, U32, "xt_w")
         fetch_wc(3)
+        for u in range(2):
+            place_wc(nc.vector.tensor_copy, u, 3, 4)
+        for u in range(2, PACK):
+            place_wc(nc.scalar.copy, u, 2, 4)
+
         wc_w = [keep.tile([P, P], U32, name="wc_w%d" % u, align_bytes=64) for u in range(PACK)]
         wc_s = [keep.tile([P, P], U8, name="wc_s%d" % u, align_bytes=64) for u in range(PACK)]
-        a_sb = [keep.tile([P, J], F32, name="a_sb%d" % u) for u in range(PACK)]
+        low = keep.tile([P, 2, J], F32, name="low")
+        high = keep.tile([P, 2, J], F32, name="high")
+        a2 = keep.tile([P, J], F32, name="a2")
+        a3 = keep.tile([P, J], F32, name="a3", tag="late", align_bytes=64)
+        a_sb = [low[:, 1, :], low[:, 0, :], a2[:], a3[:]]
+        found = [low[:, 0, :], low[:, 1, :], high[:, 0, :], high[:, 1, :]]
 
-        def first_product(u):
+        for u in range(PACK):
             nc.vector.quantize_mx(wc_w[u][:].bitcast(FP8X4), wc_s[u][:], wc_in[u][:].rearrange("p m t -> p (m t)"))
             nc.tensor.matmul_mx(acc[u][:], lhsT=wc_w[u][:].bitcast(FP8X4), lhsT_scale=wc_s[u][:],
-                                rhs=xt_w[:].bitcast(FP8X4), rhs_scale=xt_s[:], start=False, stop=True)
-            nc.scalar.copy(a_sb[u][:], acc[u][:])
+                                rhs=xt_w[:].bitcast(FP8X4), rhs_scale=xt_s[XT0 % QUAD :, :], start=False, stop=True)
+            if u in (0,):
+                nc.vector.tensor_copy(a_sb[u], acc[u][:])
+            else:
+                nc.scalar.copy(a_sb[u], acc[u][:])
 
-        place_wc(3, 0)
-        for u in range(PACK):
-            if u + 1 < PACK:
-                place_wc(3, u + 1)
-            first_product(u)
-
-        one = keep.tile([P, PACK, O], F32, name="one")
-        eight = keep.tile([P, PACK, O], F32, name="eight")
-        hid_in = keep.tile([P, O, PACK], BF16, name="hid_in", align_bytes=64)
 
         def scatter(u, engine, lo=0, hi=J):
             window = board[u][:].indirect(list4[:, lo // 16 : hi // 16])
@@ -167,25 +167,25 @@ def tile_picked_tokens_codes_bank_boardmixed_store_plain_kernel(
                 nc.scalar.activation(window, a_sb[u][:, lo:hi], COPY)
 
         def read_board(u):
-            nc.scalar.activation(one[:, u, :], board[u][:].indirect(list5[:]), COPY, scale=sa_t[:, u : u + 1])
-            nc.scalar.activation(eight[:, u, :], board[u][:].indirect(list6[:]), COPY, scale=sb_t[:, u : u + 1])
+            nc.scalar.activation(found[u][:, :O], board[u][:].indirect(list5[:]), COPY, scale=sa_t[:, u : u + 1])
+            nc.scalar.activation(found[u][:, O:], board[u][:].indirect(list6[:]), COPY, scale=sb_t[:, u : u + 1])
 
-        def larger(u):
-            nc.vector.tensor_tensor(hid_in[:, :, u], one[:, u, :], eight[:, u, :], MAX)
+        def larger(pair, u):
+            both = pair[:].rearrange("p u (s o) -> p s o u", s=2)
+            nc.vector.tensor_tensor(hid_in[:, :, u : u + 2], both[:, 0], both[:, 1], MAX)
 
         scatter(0, "vector")
-        scatter(3, "scalar")
-        spread_scale_rows(vs_plane, vs_rows)
-        scatter(1, "vector")
-        read_board(0)
-        read_board(3)
+        scatter(1, "scalar")
         scatter(2, "vector")
+        read_board(0)
         read_board(1)
-        vs_s = gather(vs_plane, list7, U8, "vs_s")
-        vs_w = gather(vs_all, list7, U32, "vs_w")
+        scatter(3, "vector", 0, 256)
         read_board(2)
-        for u in (0, 3, 1, 2):
-            larger(u)
+        vs_w = gather(vs_all, list7, U32, "vs_w", tag="late")
+        hid_in = keep.tile([P, O, PACK], BF16, name="hid_in", tag="vs_all", align_bytes=64)
+        larger(low, 0)
+        read_board(3)
+        larger(high, 2)
 
         hid_w = keep.tile([P, O], U32, name="hid_w", align_bytes=64)
         hid_s = keep.tile([P, O], U8, name="hid_s", align_bytes=64)
@@ -193,7 +193,7 @@ def tile_picked_tokens_codes_bank_boardmixed_store_plain_kernel(
         y = psum.tile([P, N // P, O], F32, name="y")
         for h in range(N // P):
             cols = slice(h * P, (h + 1) * P)
-            nc.tensor.matmul_mx(y[:, h, :], lhsT=vs_w[:, cols].bitcast(FP8X4), lhsT_scale=vs_s[:, cols],
+            nc.tensor.matmul_mx(y[:, h, :], lhsT=vs_w[:, cols].bitcast(FP8X4), lhsT_scale=vs_s[VS0 % QUAD :, cols],
                                 rhs=hid_w[:].bitcast(FP8X4), rhs_scale=hid_s[:], start=True, stop=True)
         y_sb = keep.tile([P, N // P, O], F32, name="y_sb")
         nc.vector.tensor_copy(y_sb[:], y[:])

@@ -76,12 +76,12 @@ def tile_picked_tokens_codes_bank_boardmixed_store_plain_kernel(
         w2_rows = load_scale_rows(w2_scales, R, W20, "w2_rows")
         xt_rows = load_scale_rows(xt_scales, T, XT0, "xt_rows")
         vs_rows = load_scale_rows(vs_scales, S, VS0, "vs_rows")
-        ua_tiles = [load_ua(0)]
         list2 = load_list(offs2, "list2")
         ha_t = load_column(ha, "ha_t")
         list3 = load_list(offs3, "list3")
         list1 = load_list(offs, "list1")
         list7 = load_list(offs7, "list7")
+        ua_tiles = [load_ua(0)]
         ua_tiles.append(load_ua(1))
         xo_all = load_words(xo_words[0], U16, M, "xo_all")
         w2_all = load_words(w2_words[0].rearrange(e4m3_words), U32, R, "w2_all")
@@ -107,7 +107,7 @@ def tile_picked_tokens_codes_bank_boardmixed_store_plain_kernel(
         vs_s = gather(spread_scale_rows(vs_rows, "vs_plane"), list7, U8, "vs_s")
 
         wc_planes = keep.tile([P, PACK, R], BF16, name="wc_planes")
-        wc_in = [keep.tile([P, P, PACK], BF16, name="wc_in%d" % u, align_bytes=64) for u in range(PACK)]
+        wc_in = [keep.tile([P, P, PACK], BF16, name="wc_in%d" % u, tag="wc_in%d" % u, align_bytes=64) for u in range(PACK)]
         dealt = wc_planes[:].rearrange("p t (m u) -> p u m t", u=PACK)
 
         def fetch_wc(t):
@@ -120,11 +120,11 @@ def tile_picked_tokens_codes_bank_boardmixed_store_plain_kernel(
         xo_w = gather(xo_all, list3, U16, "xo_w")
         fetch_wc(1)
         for u in range(PACK):
-            place_wc(nc.vector.tensor_copy, u, 0, 2)
-        w2_w = keep.tile([P, PACK, P], I32, name="w2_w", align_bytes=64)
-        nc.vector.tensor_copy(
+            place_wc(nc.vector.tensor_copy if u < 2 else nc.scalar.copy, u, 0, 2)
+        w2_w = keep.tile([P, PACK, P], U32, name="w2_w", align_bytes=64)
+        nc.scalar.copy(
             w2_w[:].rearrange("p t (a m) -> p a t m", m=PACK),
-            w2_all[:].bitcast(I32).rearrange("p (a m t) -> p a t m", m=PACK, t=PACK),
+            w2_all[:].rearrange("p (a m t) -> p a t m", m=PACK, t=PACK),
         )
         acc = [psum.tile([P, J], F32, name="acc%d" % u) for u in range(PACK)]
         for u in range(PACK):
@@ -143,21 +143,20 @@ def tile_picked_tokens_codes_bank_boardmixed_store_plain_kernel(
         wc_w = [keep.tile([P, P], U32, name="wc_w%d" % u, align_bytes=64) for u in range(PACK)]
         wc_s = [keep.tile([P, P], U8, name="wc_s%d" % u, align_bytes=64) for u in range(PACK)]
         low = keep.tile([P, 2, J], F32, name="low")
-        high = keep.tile([P, 2, J], F32, name="high")
-        a2 = keep.tile([P, J], F32, name="a2")
-        a3 = keep.tile([P, J], F32, name="a3", tag="late", align_bytes=64)
-        a_sb = [low[:, 1, :], low[:, 0, :], a2[:], a3[:]]
+        SPLIT = 160
+        relay = keep.tile([P, SPLIT + 2 * J], F32, name="relay")
+        high = relay[:, SPLIT:].rearrange("p (u j) -> p u j", u=2)
         found = [low[:, 0, :], low[:, 1, :], high[:, 0, :], high[:, 1, :]]
+        a2 = keep.tile([P, J], F32, name="a2", tag="a2", align_bytes=64)
+        a_sb = [relay[:, :J], low[:, 1, :], a2[:], relay[:, :J]]
 
         for u in range(PACK):
             nc.vector.quantize_mx(wc_w[u][:].bitcast(FP8X4), wc_s[u][:], wc_in[u][:].rearrange("p m t -> p (m t)"))
             nc.tensor.matmul_mx(acc[u][:], lhsT=wc_w[u][:].bitcast(FP8X4), lhsT_scale=wc_s[u][:],
                                 rhs=xt_w[:].bitcast(FP8X4), rhs_scale=xt_s[XT0 % QUAD :, :], start=False, stop=True)
-            if u in (0,):
-                nc.vector.tensor_copy(a_sb[u], acc[u][:])
-            else:
-                nc.scalar.copy(a_sb[u], acc[u][:])
 
+        def leave_psum(u, copy):
+            copy(a_sb[u], acc[u][:])
 
         def scatter(u, engine, lo=0, hi=J):
             window = board[u][:].indirect(list4[:, lo // 16 : hi // 16])
@@ -171,30 +170,35 @@ def tile_picked_tokens_codes_bank_boardmixed_store_plain_kernel(
             nc.scalar.activation(found[u][:, O:], board[u][:].indirect(list6[:]), COPY, scale=sb_t[:, u : u + 1])
 
         def larger(pair, u):
-            both = pair[:].rearrange("p u (s o) -> p s o u", s=2)
+            both = pair.rearrange("p u (s o) -> p s o u", s=2)
             nc.vector.tensor_tensor(hid_in[:, :, u : u + 2], both[:, 0], both[:, 1], MAX)
 
-        scatter(0, "vector")
-        scatter(1, "scalar")
-        scatter(2, "vector")
+        leave_psum(0, nc.scalar.copy)
+        scatter(0, "scalar")
+        leave_psum(1, nc.vector.tensor_copy)
+        leave_psum(2, nc.vector.tensor_copy)
+        scatter(1, "vector")
+        leave_psum(3, nc.scalar.copy)
         read_board(0)
+        scatter(2, "vector")
+        scatter(3, "scalar", SPLIT, J)
+        scatter(3, "vector", 0, SPLIT)
         read_board(1)
-        scatter(3, "vector", 0, 256)
         read_board(2)
-        vs_w = gather(vs_all, list7, U32, "vs_w", tag="late")
+        vs_w = gather(vs_all, list7, U32, "vs_w", tag="a2")
         hid_in = keep.tile([P, O, PACK], BF16, name="hid_in", tag="vs_all", align_bytes=64)
-        larger(low, 0)
+        larger(low[:], 0)
         read_board(3)
         larger(high, 2)
 
         hid_w = keep.tile([P, O], U32, name="hid_w", align_bytes=64)
         hid_s = keep.tile([P, O], U8, name="hid_s", align_bytes=64)
         nc.vector.quantize_mx(hid_w[:].bitcast(FP8X4), hid_s[:], hid_in[:].rearrange("p o t -> p (o t)"))
-        y = psum.tile([P, N // P, O], F32, name="y")
-        for h in range(N // P):
+        for h, (copy, queue) in enumerate(((nc.scalar.copy, nc.scalar), (nc.vector.tensor_copy, nc.sync))):
             cols = slice(h * P, (h + 1) * P)
-            nc.tensor.matmul_mx(y[:, h, :], lhsT=vs_w[:, cols].bitcast(FP8X4), lhsT_scale=vs_s[VS0 % QUAD :, cols],
+            y = psum.tile([P, O], F32, name="y%d" % h)
+            nc.tensor.matmul_mx(y[:], lhsT=vs_w[:, cols].bitcast(FP8X4), lhsT_scale=vs_s[VS0 % QUAD :, cols],
                                 rhs=hid_w[:].bitcast(FP8X4), rhs_scale=hid_s[:], start=True, stop=True)
-        y_sb = keep.tile([P, N // P, O], F32, name="y_sb")
-        nc.vector.tensor_copy(y_sb[:], y[:])
-        nc.sync.dma_start(out.rearrange("(h p) o -> p h o", p=P), y_sb[:])
+            y_sb = keep.tile([P, O], F32, name="y_sb%d" % h)
+            copy(y_sb[:], y[:])
+            queue.dma_start(out[cols, :], y_sb[:])

@@ -52,11 +52,21 @@ def tile_picked_tokens_codes_bank_boardmixed_store_plain_kernel(
             nc.scalar.dma_start(tile[first : first + PACK], src[0].bitcast(I32).rearrange("(q i) w -> i q w", i=PACK))
             return tile[base : base + QUAD]
 
-        def spread_scale_rows(rows, name):
-            plane = keep.tile([P, 4 * rows.shape[2]], U8, name=name, align_bytes=64)
+        def load_bare_scale_rows(src, width, name):
+            tile = keep.tile([PACK, PACK, width // 4], I32, name=name)
+            nc.scalar.dma_start(tile[:], src[0].bitcast(I32).rearrange("(q i) w -> i q w", i=PACK))
+            return tile[:]
+
+        def spread_scale_rows(staged):
+            planes = []
+            for rows, name in staged:
+                planes.append(keep.tile([P, 4 * rows.shape[2]], U8, name=name, align_bytes=64))
+                if rows.shape[0] < QUAD:
+                    nc.vector.memset(planes[-1][:].bitcast(I32), 0)
             for q in range(PACK):
-                nc.vector.tensor_copy(plane[:].bitcast(I32)[QUAD * q : QUAD * (q + 1), :], rows[:, q, :])
-            return plane
+                for plane, (rows, name) in zip(planes, staged):
+                    nc.vector.tensor_copy(plane[:].bitcast(I32)[QUAD * q : QUAD * q + rows.shape[0], :], rows[:, q, :])
+            return planes
 
         def gather(window, offsets, dtype, name, tag=None):
             picked = keep.tile([P, 16 * offsets.shape[1]], dtype, name=name, tag=tag or name, align_bytes=64)
@@ -72,17 +82,17 @@ def tile_picked_tokens_codes_bank_boardmixed_store_plain_kernel(
 
         XO0, W20, XT0, VS0 = 0, 64, 4, 8
         e4m3_words = "p n t -> p (n t)"
-        xo_rows = load_scale_rows(xo_scales, M, XO0, "xo_rows")
-        w2_rows = load_scale_rows(w2_scales, R, W20, "w2_rows")
+        xo_rows = load_bare_scale_rows(xo_scales, M, "xo_rows")
         xt_rows = load_scale_rows(xt_scales, T, XT0, "xt_rows")
         vs_rows = load_scale_rows(vs_scales, S, VS0, "vs_rows")
+        w2_rows = load_scale_rows(w2_scales, R, W20, "w2_rows")
         list2 = load_list(offs2, "list2")
         ha_t = load_column(ha, "ha_t")
         list3 = load_list(offs3, "list3")
-        list1 = load_list(offs, "list1")
-        list7 = load_list(offs7, "list7")
         ua_tiles = [load_ua(0)]
         ua_tiles.append(load_ua(1))
+        list1 = load_list(offs, "list1")
+        list7 = load_list(offs7, "list7")
         xo_all = load_words(xo_words[0], U16, M, "xo_all")
         w2_all = load_words(w2_words[0].rearrange(e4m3_words), U32, R, "w2_all")
         ua_tiles.append(load_ua(2))
@@ -99,12 +109,13 @@ def tile_picked_tokens_codes_bank_boardmixed_store_plain_kernel(
         for t in range(PACK):
             nc.vector.memset(board[t][:], 0.0)
 
-        xo_s = gather(spread_scale_rows(xo_rows, "xo_plane"), list3, U8, "xo_s")
-        w2_plane = spread_scale_rows(w2_rows, "w2_plane")
+        xo_plane, xt_plane, vs_plane = spread_scale_rows([(xo_rows, "xo_plane"), (xt_rows, "xt_plane"), (vs_rows, "vs_plane")])
+        (w2_plane,) = spread_scale_rows([(w2_rows, "w2_plane")])
+        xo_s = gather(xo_plane, list3, U8, "xo_s")
         w2_s = keep.tile([P, PACK, P], U8, name="w2_s", align_bytes=64)
         nc.vector.tensor_copy(w2_s[:], w2_plane[:].rearrange("p (m t) -> p t m", t=PACK))
-        xt_s = gather(spread_scale_rows(xt_rows, "xt_plane"), list1, U8, "xt_s")
-        vs_s = gather(spread_scale_rows(vs_rows, "vs_plane"), list7, U8, "vs_s")
+        xt_s = gather(xt_plane, list1, U8, "xt_s")
+        vs_s = gather(vs_plane, list7, U8, "vs_s")
 
         wc_planes = keep.tile([P, PACK, R], BF16, name="wc_planes")
         wc_in = [keep.tile([P, P, PACK], BF16, name="wc_in%d" % u, tag="wc_in%d" % u, align_bytes=64) for u in range(PACK)]
@@ -120,7 +131,7 @@ def tile_picked_tokens_codes_bank_boardmixed_store_plain_kernel(
         xo_w = gather(xo_all, list3, U16, "xo_w")
         fetch_wc(1)
         for u in range(PACK):
-            place_wc(nc.vector.tensor_copy if u < 2 else nc.scalar.copy, u, 0, 2)
+            place_wc(nc.scalar.copy, u, 0, 2)
         w2_w = keep.tile([P, PACK, P], U32, name="w2_w", align_bytes=64)
         nc.scalar.copy(
             w2_w[:].rearrange("p t (a m) -> p a t m", m=PACK),

from contextlib import ExitStack

import concourse.mybir as mybir

K, J, R, T, F, M, C, O, N, S = 512, 256, 512, 512, 2048, 1024, 512, 128, 256, 1024
FLOPS = 2 * (K * R * J + 512 * R * J + R * N * O)

F32 = mybir.dt.float32
BF16 = mybir.dt.bfloat16
I32 = mybir.dt.int32
U32 = mybir.dt.uint32
U16 = mybir.dt.uint16
U8 = mybir.dt.uint8
FP8X4 = mybir.dt.float8_e4m3fn_x4
FP4X4 = mybir.dt.float4_e2m1fn_x4
COPY = mybir.ActivationFunctionType.Copy
MAX = mybir.AluOpType.max

P = 128
PACK = 4
QUAD = 32


def tile_picked_tokens_codes_bank_boardmixed_store_plain_kernel(
    tc, xt_words, xt_scales, ua, ha, xo_words, xo_scales, w2_words, w2_scales, sa, sb, vs_words, vs_scales,
    offs, offs2, offs3, offs4, offs5, offs6, offs7, out,
):
    nc = tc.nc
    with ExitStack() as ctx:
        keep = ctx.enter_context(tc.tile_pool(name="keep", bufs=1))
        psum = ctx.enter_context(tc.psum_pool(name="psum", bufs=1))

        def load_list(src, name):
            tile = keep.tile(list(src.shape), U16, name=name)
            nc.sync.dma_start(tile[:], src)
            return tile

        def load_column(src, name):
            tile = keep.tile([P, PACK], F32, name=name)
            nc.sync.dma_start(tile[:], src.rearrange("(p t) o -> p (t o)", t=PACK))
            return tile

        def load_words(src, dtype, width, name):
            tile = keep.tile([P, width], dtype, name=name, tag=name, align_bytes=64)
            nc.sync.dma_start(tile[:].bitcast(I32), src.bitcast(I32))
            return tile

        def load_scale_rows(src, width, first, name):
            tile = keep.tile([P, PACK, width // 4], I32, name=name)
            base = first // QUAD * QUAD
            nc.vector.memset(tile[base : base + QUAD], 0)
            nc.scalar.dma_start(tile[first : first + PACK], src[0].bitcast(I32).rearrange("(q i) w -> i q w", i=PACK))
            return tile[base : base + QUAD]

        def load_bare_scale_rows(src, width, name):
            tile = keep.tile([PACK, PACK, width // 4], I32, name=name)
            nc.scalar.dma_start(tile[:], src[0].bitcast(I32).rearrange("(q i) w -> i q w", i=PACK))
            return tile[:]

        def spread_scale_rows(staged):
            planes = []
            for rows, name in staged:
                planes.append(keep.tile([P, 4 * rows.shape[2]], U8, name=name, align_bytes=64))
                if rows.shape[0] < QUAD:
                    nc.vector.memset(planes[-1][:].bitcast(I32), 0)
            for q in range(PACK):
                for plane, (rows, name) in zip(planes, staged):
                    nc.vector.tensor_copy(plane[:].bitcast(I32)[QUAD * q : QUAD * q + rows.shape[0], :], rows[:, q, :])
            return planes

        def gather(window, offsets, dtype, name, tag=None):
            picked = keep.tile([P, 16 * offsets.shape[1]], dtype, name=name, tag=tag or name, align_bytes=64)
            nc.vector.tensor_copy(picked[:], window[:].indirect(offsets[:]))
            return picked

        ua_rows = ua.rearrange("(p t) f -> t p f", t=PACK)

        def load_ua(t):
            tile = keep.tile([P, F], F32, name="ua%d" % t)
            nc.sync.dma_start(tile[:], ua_rows[t])
            return tile

        XO0, W20, XT0, VS0 = 0, 64, 4, 8
        e4m3_words = "p n t -> p (n t)"
        xo_rows = load_bare_scale_rows(xo_scales, M, "xo_rows")
        xt_rows = load_scale_rows(xt_scales, T, XT0, "xt_rows")
        vs_rows = load_scale_rows(vs_scales, S, VS0, "vs_rows")
        w2_rows = load_scale_rows(w2_scales, R, W20, "w2_rows")
        list2 = load_list(offs2, "list2")
        ha_t = load_column(ha, "ha_t")
        list3 = load_list(offs3, "list3")
        ua_tiles = [load_ua(0)]
        ua_tiles.append(load_ua(1))
        list1 = load_list(offs, "list1")
        list7 = load_list(offs7, "list7")
        xo_all = load_words(xo_words[0], U16, M, "xo_all")
        w2_all = load_words(w2_words[0].rearrange(e4m3_words), U32, R, "w2_all")
        ua_tiles.append(load_ua(2))
        ua_tiles.append(load_ua(3))
        xt_all = load_words(xt_words[0].rearrange(e4m3_words), U32, T, "xt_all")
        list4 = load_list(offs4, "list4")
        sa_t = load_column(sa, "sa_t")
        sb_t = load_column(sb, "sb_t")
        list5 = load_list(offs5, "list5")
        list6 = load_list(offs6, "list6")
        vs_all = load_words(vs_words[0].rearrange(e4m3_words), U32, S, "vs_all")

        board = [keep.tile([P, C], F32, name="board%d" % t) for t in range(PACK)]
        for t in range(PACK):
            nc.vector.memset(board[t][:], 0.0)

        xo_plane, xt_plane, vs_plane = spread_scale_rows([(xo_rows, "xo_plane"), (xt_rows, "xt_plane"), (vs_rows, "vs_plane")])
        (w2_plane,) = spread_scale_rows([(w2_rows, "w2_plane")])
        xo_s = gather(xo_plane, list3, U8, "xo_s")
        w2_s = keep.tile([P, PACK, P], U8, name="w2_s", align_bytes=64)
        nc.vector.tensor_copy(w2_s[:], w2_plane[:].rearrange("p (m t) -> p t m", t=PACK))
        xt_s = gather(xt_plane, list1, U8, "xt_s")
        vs_s = gather(vs_plane, list7, U8, "vs_s")

        wc_planes = keep.tile([P, PACK, R], BF16, name="wc_planes")
        wc_in = [keep.tile([P, P, PACK], BF16, name="wc_in%d" % u, tag="wc_in%d" % u, align_bytes=64) for u in range(PACK)]
        dealt = wc_planes[:].rearrange("p t (m u) -> p u m t", u=PACK)

        def fetch_wc(t):
            nc.scalar.activation(wc_planes[:, t, :], ua_tiles[t][:].indirect(list2[:]), COPY, scale=ha_t[:, t : t + 1])

        def place_wc(copy, u, lo, hi):
            copy(wc_in[u][:, :, lo:hi], dealt[:, u, :, lo:hi])

        fetch_wc(0)
        xo_w = gather(xo_all, list3, U16, "xo_w")
        fetch_wc(1)
        for u in range(PACK):
            place_wc(nc.scalar.copy, u, 0, 2)
        w2_w = keep.tile([P, PACK, P], U32, name="w2_w", align_bytes=64)
        nc.scalar.copy(
            w2_w[:].rearrange("p t (a m) -> p a t m", m=PACK),
            w2_all[:].rearrange("p (a m t) -> p a t m", m=PACK, t=PACK),
        )
        acc = [psum.tile([P, J], F32, name="acc%d" % u) for u in range(PACK)]
        for u in range(PACK):
            nc.tensor.matmul_mx(acc[u][:], lhsT=w2_w[:, u, :].bitcast(FP8X4), lhsT_scale=w2_s[:, u, :],
                                rhs=xo_w[:].bitcast(FP4X4), rhs_scale=xo_s[:], start=True, stop=False)
        fetch_wc(2)
        for u in range(2):
            place_wc(nc.vector.tensor_copy, u, 2, 3)
        xt_w = gather(xt_all, list1, U32, "xt_w")
        fetch_wc(3)
        for u in range(2):
            place_wc(nc.vector.tensor_copy, u, 3, 4)
        for u in range(2, PACK):
            place_wc(nc.scalar.copy, u, 2, 4)

        wc_w = [keep.tile([P, P], U32, name="wc_w%d" % u, align_bytes=64) for u in range(PACK)]
        wc_s = [keep.tile([P, P], U8, name="wc_s%d" % u, align_bytes=64) for u in range(PACK)]
        low = keep.tile([P, 2, J], F32, name="low")
        SPLIT = 160
        relay = keep.tile([P, SPLIT + 2 * J], F32, name="relay")
        high = relay[:, SPLIT:].rearrange("p (u j) -> p u j", u=2)
        found = [low[:, 0, :], low[:, 1, :], high[:, 0, :], high[:, 1, :]]
        a2 = keep.tile([P, J], F32, name="a2", tag="a2", align_bytes=64)
        a_sb = [relay[:, :J], low[:, 1, :], a2[:], relay[:, :J]]

        for u in range(PACK):
            nc.vector.quantize_mx(wc_w[u][:].bitcast(FP8X4), wc_s[u][:], wc_in[u][:].rearrange("p m t -> p (m t)"))
            nc.tensor.matmul_mx(acc[u][:], lhsT=wc_w[u][:].bitcast(FP8X4), lhsT_scale=wc_s[u][:],
                                rhs=xt_w[:].bitcast(FP8X4), rhs_scale=xt_s[XT0 % QUAD :, :], start=False, stop=True)

        def leave_psum(u, copy):
            copy(a_sb[u], acc[u][:])

        def scatter(u, engine, lo=0, hi=J):
            window = board[u][:].indirect(list4[:, lo // 16 : hi // 16])
            if engine == "vector":
                nc.vector.tensor_copy(window, a_sb[u][:, lo:hi])
            else:
                nc.scalar.activation(window, a_sb[u][:, lo:hi], COPY)

        def read_board(u):
            nc.scalar.activation(found[u][:, :O], board[u][:].indirect(list5[:]), COPY, scale=sa_t[:, u : u + 1])
            nc.scalar.activation(found[u][:, O:], board[u][:].indirect(list6[:]), COPY, scale=sb_t[:, u : u + 1])

        def larger(pair, u):
            both = pair.rearrange("p u (s o) -> p s o u", s=2)
            nc.vector.tensor_tensor(hid_in[:, :, u : u + 2], both[:, 0], both[:, 1], MAX)

        leave_psum(0, nc.scalar.copy)
        scatter(0, "scalar")
        leave_psum(1, nc.vector.tensor_copy)
        leave_psum(2, nc.vector.tensor_copy)
        scatter(1, "vector")
        leave_psum(3, nc.scalar.copy)
        read_board(0)
        scatter(2, "vector")
        scatter(3, "scalar", SPLIT, J)
        scatter(3, "vector", 0, SPLIT)
        read_board(1)
        read_board(2)
        vs_w = gather(vs_all, list7, U32, "vs_w", tag="a2")
        hid_in = keep.tile([P, O, PACK], BF16, name="hid_in", tag="vs_all", align_bytes=64)
        larger(low[:], 0)
        read_board(3)
        larger(high, 2)

        hid_w = keep.tile([P, O], U32, name="hid_w", align_bytes=64)
        hid_s = keep.tile([P, O], U8, name="hid_s", align_bytes=64)
        nc.vector.quantize_mx(hid_w[:].bitcast(FP8X4), hid_s[:], hid_in[:].rearrange("p o t -> p (o t)"))
        for h, (copy, queue) in enumerate(((nc.scalar.copy, nc.scalar), (nc.vector.tensor_copy, nc.sync))):
            cols = slice(h * P, (h + 1) * P)
            y = psum.tile([P, O], F32, name="y%d" % h)
            nc.tensor.matmul_mx(y[:], lhsT=vs_w[:, cols].bitcast(FP8X4), lhsT_scale=vs_s[VS0 % QUAD :, cols],
                                rhs=hid_w[:].bitcast(FP8X4), rhs_scale=hid_s[:], start=True, stop=True)
            y_sb = keep.tile([P, O], F32, name="y_sb%d" % h)
            copy(y_sb[:], y[:])
            queue.dma_start(out[cols, :], y_sb[:])
